import numpy as np
import ml_dtypes


def mxq(x, axis, fmt="e4m3"):
    dtype, down = {"e4m3": (ml_dtypes.float8_e4m3fn, 7), "e5m2": (ml_dtypes.float8_e5m2, 14)}[fmt]
    v = np.moveaxis(np.asarray(x, np.float32).astype(ml_dtypes.bfloat16).astype(np.float64), axis, -1)
    blocks = v.reshape(v.shape[:-1] + (-1, 32))
    amax = np.abs(blocks).max(-1, keepdims=True)
    byte = np.maximum(np.where(amax > 0, np.frexp(amax)[1] - 1 + 127, 0) - down, 1)
    scale = np.exp2(byte - 127.0)
    codes = (blocks / scale).astype(np.float32).astype(dtype).astype(np.float64)
    return np.moveaxis((codes * scale).reshape(v.shape), -1, axis)


WIDE = False


def mx_kscale(k):
    if not WIDE:
        return np.ones(k)
    levels = np.array([10, -10, 5, -5, 0])
    if k % 512:
        return np.exp2(np.random.permutation(np.resize(levels, k // 32))).repeat(32)
    a = np.empty((k // 512, 16))
    for p in range(k // 512):
        a[p, :8] = np.random.permutation(np.resize(levels, 8))
        for g in range(8):
            far = levels[np.abs(levels - a[p, g]) >= 10]
            a[p, g + 8] = far[np.random.randint(len(far))]
    return np.exp2(a.ravel()).repeat(32)


def f64(x):
    return np.asarray(x).astype(np.float64)


def striped(idx):
    return np.tile(idx.reshape(-1, 16).T, (8, 1)).astype(np.uint16)


def unstriped(offs):
    return offs[:16].T.reshape(-1).astype(np.int64)


def striped8(idx):
    return np.concatenate([x.reshape(-1, 16).T for x in idx]).astype(np.uint16)


def runs(offs, k):
    lists = np.stack([offs[16 * r : 16 * r + 16].T.reshape(-1) for r in range(8)]).astype(np.int64)
    return lists[np.arange(k) % 512 // 64]


def pack_weight(w):
    k, n = w.shape
    w = f64(np.asarray(w, np.float32).astype(ml_dtypes.bfloat16)).reshape(k // 32, 32, n)
    amax = np.abs(w).max(1)
    byte = np.clip(np.where(amax > 0, np.frexp(amax)[1] - 1 + 127 - 7, 1), 1, 254)
    scaled = (w * np.exp2(127.0 - byte)[:, None, :]).reshape(k, n).astype(np.float32)
    words = np.ascontiguousarray(scaled.reshape(k // 512, 128, 4, n).transpose(0, 1, 3, 2)).astype(ml_dtypes.float8_e4m3fn).view(np.uint8)
    return words, np.ascontiguousarray(byte.astype(np.uint8).reshape(k // 512, 16, n))


def unpack_weight(words, scales):
    g, p, n, _ = words.shape
    vals = np.ascontiguousarray(words).view(ml_dtypes.float8_e4m3fn).astype(np.float64) * np.repeat(np.exp2(scales.astype(np.float64) - 127.0), 8, axis=1)[..., None]
    return vals.transpose(0, 1, 3, 2).reshape(g * 512, n)


def relu(v):
    return np.maximum(v, 0.0)


K, T, S, V, N, W, H = 512, 2048, 512, 512, 512, 1024, 512


def setup_inputs():
    n = np.random.standard_normal
    s = mx_kscale(K)[:, None]
    u = mx_kscale(H)
    packed_xT = pack_weight(n((K, T)) * s)
    return {
        "x_words": packed_xT[0],
        "x_scales": packed_xT[1],
        "w1": (n((K, H)) / np.sqrt(K) / s * u).astype(np.float32),
        "w2": (n((H, H)) / np.sqrt(2 * H) / u[:, None] * u).astype(np.float32),
        "w3": (n((K, H)) / np.sqrt(2 * K) / s * u).astype(np.float32),
        "w4": (n((H, N)) / np.sqrt(2 * H) / u[:, None]).astype(np.float32),
        "w5": (n((K, N)) / np.sqrt(2 * K) / s).astype(np.float32),
        "offs": striped(np.random.permutation(T)[:S]),
        "par": striped8(np.random.randint(0, S, (8, V))),
        "own": striped(np.random.permutation(T)[:V]),
        "par2": striped8(np.random.randint(0, V, (8, W))),
        "leaf": striped(np.random.permutation(T)[:W]),
    }


def reference(x_words, x_scales, w1, w2, w3, w4, w5, offs, par, own, par2, leaf):
    xq = unpack_weight(x_words, x_scales)[:, unstriped(offs)]
    y = mxq(f64(w1), 0, "e4m3").T @ xq
    z = y[np.arange(H)[:, None], runs(par, H)]
    x_own = unpack_weight(x_words, x_scales)[:, unstriped(own)]
    h = relu(mxq(f64(w2), 0, "e4m3").T @ mxq(z, 0, "e4m3") + mxq(f64(w3), 0, "e4m3").T @ x_own)
    z2 = h[np.arange(H)[:, None], runs(par2, H)]
    x_leaf = unpack_weight(x_words, x_scales)[:, unstriped(leaf)]
    return mxq(f64(w4), 0, "e4m3").T @ mxq(z2, 0, "e4m3") + mxq(f64(w5), 0, "e4m3").T @ x_leaf

@@ -1,0 +1,194 @@
+from contextlib import ExitStack
+
+import concourse.mybir as mybir
+
+F32 = mybir.dt.float32
+BF16 = mybir.dt.bfloat16
+I32 = mybir.dt.int32
+U32 = mybir.dt.uint32
+U16 = mybir.dt.uint16
+U8 = mybir.dt.uint8
+FP8X4 = mybir.dt.float8_e4m3fn_x4
+RELU = mybir.ActivationFunctionType.Relu
+
+P = 128
+PACK = 4
+GROUP = 16
+T, S, V, W, H = 2048, 512, 512, 1024, 512
+FLOPS = 2 * 512 * 512 * (S + 2 * V + 2 * W)
+
+NODE_CHUNKS = [(0, 256), (256, 256)]
+LEAF_CHUNKS = [(0, 256), (256, 256), (512, 256), (768, 128), (896, 128)]
+
+
+def tile_picked_topdn2_relu_p_kernel(tc, x_words, x_scales, w1, w2, w3, w4, w5, offs, par, own, par2, leaf, out):
+    nc = tc.nc
+    with ExitStack() as ctx:
+        lists = ctx.enter_context(tc.tile_pool(name="lists", bufs=1))
+        keep = ctx.enter_context(tc.tile_pool(name="keep", bufs=1))
+        ring = ctx.enter_context(tc.tile_pool(name="ring", bufs=2))
+        psum = ctx.enter_context(tc.psum_pool(name="psum", bufs=1))
+
+        def load_list(name, source):
+            tile = lists.tile(list(source.shape), U16, name=name)
+            nc.sync.dma_start(tile[:], source)
+            return tile
+
+        def load_weight(name, source):
+            tile = keep.tile([P, PACK, H], F32, name=name + "_raw")
+            nc.sync.dma_start(tile[:], source.rearrange("(p j) c -> p j c", j=PACK))
+            return tile
+
+        def entries(tile, first, count):
+            return tile[:, first // GROUP : (first + count) // GROUP]
+
+        def cast_dealt(name, raw, tag=None):
+            tile = keep.tile([P, H * PACK], BF16, name=name + "_bf16", tag=tag or name + "_bf16", align_bytes=64)
+            nc.scalar.copy(
+                tile[:].rearrange("p (t m j) -> p m j t", t=PACK, j=PACK),
+                raw[:].rearrange("p j (m t) -> p m j t", t=PACK),
+            )
+            return tile
+
+        def cast_plain(name, raw, copy, tag=None):
+            tile = keep.tile([P, H * PACK], BF16, name=name + "_bf16", tag=tag or name + "_bf16", align_bytes=64)
+            copy(
+                tile[:].rearrange("p (c i j) -> p c j i", i=PACK, j=PACK),
+                raw[:].rearrange("p j (c i) -> p c j i", i=PACK),
+            )
+            return tile
+
+        def quantise(name, values, width):
+            codes = keep.tile([P, width], U32, name=name + "_codes", align_bytes=64)
+            scales = keep.tile([P, width], U8, name=name + "_scales", align_bytes=64)
+            nc.vector.quantize_mx(out=codes[:].bitcast(FP8X4), scales=scales[:], in_=values)
+            return codes, scales
+
+        def pick(name, table, dtype, offsets, count, tag=None):
+            tile = keep.tile([P, count], dtype, name=name, tag=tag or name, align_bytes=64)
+            nc.vector.tensor_copy(tile[:], table[:].indirect(offsets))
+            return tile
+
+        def product(bank, weight, t, codes, scales, start, stop):
+            cols = slice(t * P, (t + 1) * P)
+            nc.tensor.matmul_mx(
+                out=bank,
+                lhsT=weight[0][:, cols].bitcast(FP8X4),
+                lhsT_scale=weight[1][:, cols],
+                rhs=codes.bitcast(FP8X4),
+                rhs_scale=scales,
+                start=start,
+                stop=stop,
+            )
+
+        def fetch(pool, name, tag, rows, offsets, count):
+            planes = pool.tile([P, PACK, count], BF16, name=name, tag=tag, align_bytes=64)
+            for t in range(PACK):
+                nc.vector.tensor_copy(planes[:, t, :], rows[t][:].indirect(offsets))
+            return planes
+
+        def weave(name, planes, count, copy):
+            tile = keep.tile([P, count * PACK], BF16, name=name, align_bytes=64)
+            copy(
+                tile[:].rearrange("p (c i t) -> p c t i", i=PACK, t=PACK),
+                planes[:].rearrange("p t (c i) -> p c t i", i=PACK),
+            )
+            return tile
+
+        def banks(first):
+            return [psum.tile([P, 512], F32, name="bank", tag="bank%d" % (first + t)) for t in range(PACK)]
+
+        byte_table = keep.tile([P, T], U8)
+        nc.vector.memset(byte_table[:].bitcast(I32), 0)
+        offs_sb = load_list("offs_sb", offs)
+        leaf_sb = load_list("leaf_sb", leaf)
+        own_sb = load_list("own_sb", own)
+        for q in range(4):
+            nc.sync.dma_start(
+                byte_table[32 * q : 32 * q + 4, :].bitcast(I32), x_scales[0, 4 * q : 4 * q + 4, :].bitcast(I32)
+            )
+        w1_raw = load_weight("w1", w1)
+        w2_raw = load_weight("w2", w2)
+        word_table = keep.tile([P, T], U32)
+        nc.sync.dma_start(word_table[:].bitcast(I32), x_words[0].rearrange("p n r -> p (n r)").bitcast(I32))
+        par_sb = load_list("par_sb", par)
+        w3_raw = load_weight("w3", w3)
+        par2_sb = load_list("par2_sb", par2)
+        w4_raw = load_weight("w4", w4)
+        w5_raw = load_weight("w5", w5)
+
+        root_bytes = pick("root_bytes", byte_table, U8, offs_sb[:], S)
+        leaf_bytes = pick("leaf_bytes", byte_table, U8, leaf_sb[:], W)
+        own_bytes = pick("own_bytes", byte_table, U8, own_sb[:], V)
+        w1_bf16 = cast_dealt("w1", w1_raw)
+        w2_bf16 = cast_dealt("w2", w2_raw)
+        w1_mx = quantise("w1", w1_bf16[:], H)
+        root_words = pick("root_words", word_table, U32, offs_sb[:], S)
+
+        y_banks = banks(0)
+        y = []
+        for t in range(PACK):
+            product(y_banks[t][:], w1_mx, t, root_words[:], root_bytes[:], True, True)
+            rows = keep.tile([P, S], F32, name="y%d" % t, tag="y%d" % t, align_bytes=64)
+            nc.scalar.copy(rows[:], y_banks[t][:])
+            y.append(rows)
+
+        own_words = pick("own_words", word_table, U32, own_sb[:], V)
+        w2_mx = quantise("w2", w2_bf16[:], H)
+        w3_bf16 = cast_dealt("w3", w3_raw, tag="root_words")
+
+        z_planes = []
+        for c, (first, count) in enumerate(NODE_CHUNKS):
+            z_planes.append(fetch(keep, "z_planes", "z_planes%d" % c, y, entries(par_sb, first, count), count))
+        w3_mx = quantise("w3", w3_bf16[:], H)
+
+        h = [keep.tile([P, V], F32, name="h%d" % t) for t in range(PACK)]
+        leaf_words = []
+        for c, (first, count) in enumerate(NODE_CHUNKS):
+            woven = weave("z_woven%d" % c, z_planes[c], count, nc.scalar.copy)
+            z_codes, z_scales = quantise("z%d" % c, woven[:], count)
+            leaf_words.append(
+                pick("leaf_words", word_table, U32, entries(leaf_sb, 512 * c, 512), 512, tag=["y2", "z_planes1"][c])
+            )
+            h_banks = banks(4 - 4 * c)
+            cols = slice(first, first + count)
+            for t in range(PACK):
+                product(h_banks[t][:, :count], w3_mx, t, own_words[:, cols], own_bytes[:, cols], True, False)
+            for t in range(PACK):
+                product(h_banks[t][:, :count], w2_mx, t, z_codes[:], z_scales[:], False, True)
+                nc.scalar.activation(h[t][:, cols], h_banks[t][:, :count], RELU)
+
+        w4_bf16 = cast_plain("w4", w4_raw, nc.scalar.copy, tag="z1_codes")
+        w5_bf16 = cast_plain("w5", w5_raw, nc.vector.tensor_copy)
+        w4_mx = quantise("w4", w4_bf16[:], H)
+        w5_mx = quantise("w5", w5_bf16[:], H)
+
+        out_rows = out.rearrange("(t p) q -> p t q", p=P)
+
+        def finish(c, woven):
+            first, count = LEAF_CHUNKS[c]
+            last = c == len(LEAF_CHUNKS) - 1
+            z2_codes, z2_scales = quantise("z2_%d" % c, woven[:], count)
+            out_banks = banks(4 - 4 * (c % 2))
+            words = leaf_words[first // 512][:, first % 512 : first % 512 + count]
+            for t in range(PACK):
+                product(out_banks[t][:, :count], w5_mx, t, words, leaf_bytes[:, first : first + count], True, False)
+            result = keep.tile([P, PACK, count], F32, name="result%d" % c)
+            for t in range(PACK):
+                product(out_banks[t][:, :count], w4_mx, t, z2_codes[:], z2_scales[:], False, True)
+                copy = nc.vector.tensor_copy if last and t % 2 else nc.scalar.copy
+                copy(result[:, t, :], out_banks[t][:, :count])
+            nc.sync.dma_start(out_rows[:, :, first : first + count], result[:])
+
+        woven = None
+        for c, (first, count) in enumerate(LEAF_CHUNKS):
+            last = c == len(LEAF_CHUNKS) - 1
+            planes = fetch(ring, "z2_planes", "z2_planes", h, entries(par2_sb, first, count), count)
+            if last:
+                finish(c - 1, woven)
+                finish(c, weave("z2_woven%d" % c, planes, count, nc.vector.tensor_copy))
+            else:
+                upcoming = weave("z2_woven%d" % c, planes, count, nc.scalar.copy)
+                if c:
+                    finish(c - 1, woven)
+                woven = upcoming

@@ -10,11 +10,13 @@ U16 = mybir.dt.uint16
 U8 = mybir.dt.uint8
 FP8X4 = mybir.dt.float8_e4m3fn_x4
 RELU = mybir.ActivationFunctionType.Relu
+MULT = mybir.AluOpType.mult
+ADD = mybir.AluOpType.add
 
 P = 128
 PACK = 4
-GROUP = 16
 T, S, V, W, H = 2048, 512, 512, 1024, 512
+LIST_ROWS = 16
 FLOPS = 2 * 512 * 512 * (S + 2 * V + 2 * W)
 
 NODE_CHUNKS = [(0, 256), (256, 256)]
@@ -26,169 +28,187 @@ def tile_picked_topdn2_relu_p_kernel(tc, x_words, x_scales, w1, w2, w3, w4, w5, 
     with ExitStack() as ctx:
         lists = ctx.enter_context(tc.tile_pool(name="lists", bufs=1))
         keep = ctx.enter_context(tc.tile_pool(name="keep", bufs=1))
-        ring = ctx.enter_context(tc.tile_pool(name="ring", bufs=2))
         psum = ctx.enter_context(tc.psum_pool(name="psum", bufs=1))
+
+        def sbuf(name, width, dtype, slot=None):
+            return keep.tile([P, width], dtype, name=name, tag=slot or name, align_bytes=64)
 
         def load_list(name, source):
             tile = lists.tile(list(source.shape), U16, name=name)
             nc.sync.dma_start(tile[:], source)
             return tile
 
-        def load_weight(name, source):
-            tile = keep.tile([P, PACK, H], F32, name=name + "_raw")
-            nc.sync.dma_start(tile[:], source.rearrange("(p j) c -> p j c", j=PACK))
+        def load_weight(name, source, first, count):
+            tile = sbuf(name, PACK * count, F32)
+            rows = tile[:].rearrange("p (j c) -> p j c", j=PACK)
+            nc.sync.dma_start(rows, source.rearrange("(p j) c -> p j c", j=PACK)[:, :, first : first + count])
             return tile
 
-        def entries(tile, first, count):
-            return tile[:, first // GROUP : (first + count) // GROUP]
-
-        def cast_dealt(name, raw, tag=None):
-            tile = keep.tile([P, H * PACK], BF16, name=name + "_bf16", tag=tag or name + "_bf16", align_bytes=64)
+        def cast_dealt(target, raw, first, count):
             nc.scalar.copy(
-                tile[:].rearrange("p (t m j) -> p m j t", t=PACK, j=PACK),
-                raw[:].rearrange("p j (m t) -> p m j t", t=PACK),
+                target.rearrange("p (t m j) -> p m j t", t=PACK, j=PACK)[:, first // PACK : (first + count) // PACK],
+                raw[:].rearrange("p (j m t) -> p m j t", j=PACK, t=PACK),
             )
-            return tile
 
-        def cast_plain(name, raw, copy, tag=None):
-            tile = keep.tile([P, H * PACK], BF16, name=name + "_bf16", tag=tag or name + "_bf16", align_bytes=64)
+        def cast_plain(target, raw, copy):
             copy(
-                tile[:].rearrange("p (c i j) -> p c j i", i=PACK, j=PACK),
-                raw[:].rearrange("p j (c i) -> p c j i", i=PACK),
+                target.rearrange("p (c i j) -> p c j i", i=PACK, j=PACK),
+                raw[:].rearrange("p (j c i) -> p c j i", j=PACK, i=PACK),
             )
-            return tile
+
+        def cast_pool(target, raw):
+            for piece in range(4):
+                cols = slice(piece * 128, (piece + 1) * 128)
+                nc.gpsimd.tensor_scalar(
+                    target.rearrange("p (c j) -> p c j", j=PACK)[:, cols],
+                    raw[:].rearrange("p (j c) -> p c j", j=PACK)[:, cols],
+                    1.0,
+                    0.0,
+                    MULT,
+                    ADD,
+                )
 
         def quantise(name, values, width):
-            codes = keep.tile([P, width], U32, name=name + "_codes", align_bytes=64)
-            scales = keep.tile([P, width], U8, name=name + "_scales", align_bytes=64)
+            codes = sbuf(name + "_codes", width, U32)
+            scales = sbuf(name + "_scales", width, U8)
             nc.vector.quantize_mx(out=codes[:].bitcast(FP8X4), scales=scales[:], in_=values)
             return codes, scales
 
-        def pick(name, table, dtype, offsets, count, tag=None):
-            tile = keep.tile([P, count], dtype, name=name, tag=tag or name, align_bytes=64)
+        def pick(name, table, dtype, offsets, count, slot=None):
+            tile = sbuf(name, count, dtype, slot)
             nc.vector.tensor_copy(tile[:], table[:].indirect(offsets))
             return tile
 
-        def product(bank, weight, t, codes, scales, start, stop):
-            cols = slice(t * P, (t + 1) * P)
+        def fetch(name, rows, offsets, first, count, slot=None):
+            planes = sbuf(name, PACK * count, BF16, slot)
+            entries = offsets[:, first // LIST_ROWS : (first + count) // LIST_ROWS]
+            for t in range(PACK):
+                nc.vector.tensor_copy(planes[:, t * count : (t + 1) * count], rows[t][:].indirect(entries))
+            return planes
+
+        def weave(target, planes, first, count, copy):
+            copy(
+                target.rearrange("p (c i t) -> p c t i", i=PACK, t=PACK),
+                planes[:].rearrange("p (t c i) -> p c t i", t=PACK, i=PACK)[:, first // PACK : (first + count) // PACK],
+            )
+
+        def product(bank, weights, column, moving, first, count, start, stop):
             nc.tensor.matmul_mx(
-                out=bank,
-                lhsT=weight[0][:, cols].bitcast(FP8X4),
-                lhsT_scale=weight[1][:, cols],
-                rhs=codes.bitcast(FP8X4),
-                rhs_scale=scales,
+                out=bank[:, :count],
+                lhsT=weights[0][:, column : column + P].bitcast(FP8X4),
+                lhsT_scale=weights[1][:, column : column + P],
+                rhs=moving[0][:, first : first + count].bitcast(FP8X4),
+                rhs_scale=moving[1][:, first : first + count],
                 start=start,
                 stop=stop,
             )
 
-        def fetch(pool, name, tag, rows, offsets, count):
-            planes = pool.tile([P, PACK, count], BF16, name=name, tag=tag, align_bytes=64)
-            for t in range(PACK):
-                nc.vector.tensor_copy(planes[:, t, :], rows[t][:].indirect(offsets))
-            return planes
-
-        def weave(name, planes, count, copy):
-            tile = keep.tile([P, count * PACK], BF16, name=name, align_bytes=64)
-            copy(
-                tile[:].rearrange("p (c i t) -> p c t i", i=PACK, t=PACK),
-                planes[:].rearrange("p t (c i) -> p c t i", i=PACK),
-            )
-            return tile
-
         def banks(first):
             return [psum.tile([P, 512], F32, name="bank", tag="bank%d" % (first + t)) for t in range(PACK)]
 
-        byte_table = keep.tile([P, T], U8)
+        half = H // 2
+        byte_table = sbuf("byte_table", T, U8)
         nc.vector.memset(byte_table[:].bitcast(I32), 0)
         offs_sb = load_list("offs_sb", offs)
         leaf_sb = load_list("leaf_sb", leaf)
-        own_sb = load_list("own_sb", own)
         for q in range(4):
             nc.sync.dma_start(
                 byte_table[32 * q : 32 * q + 4, :].bitcast(I32), x_scales[0, 4 * q : 4 * q + 4, :].bitcast(I32)
             )
-        w1_raw = load_weight("w1", w1)
-        w2_raw = load_weight("w2", w2)
-        word_table = keep.tile([P, T], U32)
+        w1_low = load_weight("w1_low", w1, 0, half)
+        w1_high = load_weight("w1_high", w1, half, half)
+        own_sb = load_list("own_sb", own)
+        word_table = sbuf("word_table", T, U32)
         nc.sync.dma_start(word_table[:].bitcast(I32), x_words[0].rearrange("p n r -> p (n r)").bitcast(I32))
+        w3_low = load_weight("w3_low", w3, 0, half)
+        w3_high = load_weight("w3_high", w3, half, half)
         par_sb = load_list("par_sb", par)
-        w3_raw = load_weight("w3", w3)
+        w2_low = load_weight("w2_low", w2, 0, half)
+        w2_high = load_weight("w2_high", w2, half, half)
         par2_sb = load_list("par2_sb", par2)
-        w4_raw = load_weight("w4", w4)
-        w5_raw = load_weight("w5", w5)
+        w4_raw = load_weight("w4_raw", w4, 0, H)
+        w5_raw = load_weight("w5_raw", w5, 0, H)
+
+        y = [sbuf("y%d" % t, 2 * S, F32) for t in range(1, PACK)]
+        for rows in y:
+            nc.vector.memset(rows[:, S:], 0.0)
 
         root_bytes = pick("root_bytes", byte_table, U8, offs_sb[:], S)
         leaf_bytes = pick("leaf_bytes", byte_table, U8, leaf_sb[:], W)
         own_bytes = pick("own_bytes", byte_table, U8, own_sb[:], V)
-        w1_bf16 = cast_dealt("w1", w1_raw)
-        w2_bf16 = cast_dealt("w2", w2_raw)
+        w1_bf16 = sbuf("w1_bf16", PACK * H, BF16)
+        cast_dealt(w1_bf16[:], w1_low, 0, half)
+        cast_dealt(w1_bf16[:], w1_high, half, half)
         w1_mx = quantise("w1", w1_bf16[:], H)
-        root_words = pick("root_words", word_table, U32, offs_sb[:], S)
+        roots = (pick("root_words", word_table, U32, offs_sb[:], S), root_bytes)
+        owns = (pick("own_words", word_table, U32, own_sb[:], V), own_bytes)
 
+        w3_bf16 = sbuf("w3_bf16", PACK * H, BF16)
+        cast_dealt(w3_bf16[:], w3_low, 0, half)
+        y = [sbuf("y0", 2 * S, F32, "w3_low")] + y
+        nc.gpsimd.memset(y[0][:, S:], 0.0)
         y_banks = banks(0)
-        y = []
         for t in range(PACK):
-            product(y_banks[t][:], w1_mx, t, root_words[:], root_bytes[:], True, True)
-            rows = keep.tile([P, S], F32, name="y%d" % t, tag="y%d" % t, align_bytes=64)
-            nc.scalar.copy(rows[:], y_banks[t][:])
-            y.append(rows)
+            product(y_banks[t], w1_mx, t * P, roots, 0, S, True, True)
+            nc.scalar.copy(y[t][:, :S], y_banks[t][:])
+        cast_dealt(w3_bf16[:], w3_high, half, half)
+        w2_bf16 = sbuf("w2_bf16", PACK * H, BF16)
+        cast_dealt(w2_bf16[:], w2_low, 0, half)
+        cast_dealt(w2_bf16[:], w2_high, half, half)
 
-        own_words = pick("own_words", word_table, U32, own_sb[:], V)
-        w2_mx = quantise("w2", w2_bf16[:], H)
-        w3_bf16 = cast_dealt("w3", w3_raw, tag="root_words")
-
-        z_planes = []
-        for c, (first, count) in enumerate(NODE_CHUNKS):
-            z_planes.append(fetch(keep, "z_planes", "z_planes%d" % c, y, entries(par_sb, first, count), count))
+        z_planes = fetch("z_planes", y, par_sb, 0, V)
         w3_mx = quantise("w3", w3_bf16[:], H)
+        leaf_words = [pick("leaf_words", word_table, U32, leaf_sb[:, : W // 2 // LIST_ROWS], W // 2, "w2_low")]
+        w2_mx = quantise("w2", w2_bf16[:], H)
 
-        h = [keep.tile([P, V], F32, name="h%d" % t) for t in range(PACK)]
-        leaf_words = []
+        h = [sbuf("h%d" % t, V, F32) for t in range(PACK)]
+        z_woven = sbuf("z_woven", PACK * V, BF16, "w2_high")
         for c, (first, count) in enumerate(NODE_CHUNKS):
-            woven = weave("z_woven%d" % c, z_planes[c], count, nc.scalar.copy)
-            z_codes, z_scales = quantise("z%d" % c, woven[:], count)
-            leaf_words.append(
-                pick("leaf_words", word_table, U32, entries(leaf_sb, 512 * c, 512), 512, tag=["y2", "z_planes1"][c])
-            )
+            woven = z_woven[:, PACK * first : PACK * (first + count)]
+            weave(woven, z_planes, first, count, nc.scalar.copy)
+            z = quantise("z%d" % c, woven, count)
             h_banks = banks(4 - 4 * c)
-            cols = slice(first, first + count)
             for t in range(PACK):
-                product(h_banks[t][:, :count], w3_mx, t, own_words[:, cols], own_bytes[:, cols], True, False)
+                product(h_banks[t], w3_mx, t * P, owns, first, count, True, False)
             for t in range(PACK):
-                product(h_banks[t][:, :count], w2_mx, t, z_codes[:], z_scales[:], False, True)
-                nc.scalar.activation(h[t][:, cols], h_banks[t][:, :count], RELU)
+                product(h_banks[t], w2_mx, t * P, z, 0, count, False, True)
+                nc.scalar.activation(h[t][:, first : first + count], h_banks[t][:, :count], RELU)
 
-        w4_bf16 = cast_plain("w4", w4_raw, nc.scalar.copy, tag="z1_codes")
-        w5_bf16 = cast_plain("w5", w5_raw, nc.vector.tensor_copy)
-        w4_mx = quantise("w4", w4_bf16[:], H)
-        w5_mx = quantise("w5", w5_bf16[:], H)
+        leaf_words.append(pick("leaf_words", word_table, U32, leaf_sb[:, W // 2 // LIST_ROWS :], W // 2, "z_planes"))
+        w45_bf16 = sbuf("w45_bf16", 2 * PACK * H, BF16, "z1_codes")
+        cast_plain(w45_bf16[:, : PACK * H], w4_raw, nc.scalar.copy)
+        cast_plain(w45_bf16[:, PACK * H :], w5_raw, nc.scalar.copy)
+        w45_mx = quantise("w45", w45_bf16[:], 2 * H)
 
         out_rows = out.rearrange("(t p) q -> p t q", p=P)
 
         def finish(c, woven):
             first, count = LEAF_CHUNKS[c]
             last = c == len(LEAF_CHUNKS) - 1
-            z2_codes, z2_scales = quantise("z2_%d" % c, woven[:], count)
+            z2 = quantise("z2_%d" % c, woven[:], count)
+            leaves = (leaf_words[first // 512][:, first % 512 :], leaf_bytes[:, first:])
             out_banks = banks(4 - 4 * (c % 2))
-            words = leaf_words[first // 512][:, first % 512 : first % 512 + count]
             for t in range(PACK):
-                product(out_banks[t][:, :count], w5_mx, t, words, leaf_bytes[:, first : first + count], True, False)
+                product(out_banks[t], w45_mx, H + t * P, leaves, 0, count, True, False)
             result = keep.tile([P, PACK, count], F32, name="result%d" % c)
             for t in range(PACK):
-                product(out_banks[t][:, :count], w4_mx, t, z2_codes[:], z2_scales[:], False, True)
+                product(out_banks[t], w45_mx, t * P, z2, 0, count, False, True)
                 copy = nc.vector.tensor_copy if last and t % 2 else nc.scalar.copy
                 copy(result[:, t, :], out_banks[t][:, :count])
-            nc.sync.dma_start(out_rows[:, :, first : first + count], result[:])
+                if last and t % 2:
+                    nc.sync.dma_start(out_rows[:, t - 1 : t + 1, first : first + count], result[:, t - 1 : t + 1, :])
+            if not last:
+                nc.sync.dma_start(out_rows[:, :, first : first + count], result[:])
 
-        woven = None
+        woven = []
         for c, (first, count) in enumerate(LEAF_CHUNKS):
             last = c == len(LEAF_CHUNKS) - 1
-            planes = fetch(ring, "z2_planes", "z2_planes", h, entries(par2_sb, first, count), count)
+            planes = fetch("z2_planes", h, par2_sb, first, count, ["z2_planes", "w4_raw"][c % 2])
+            woven.append(sbuf("z2_woven%d" % c, PACK * count, BF16))
             if last:
-                finish(c - 1, woven)
-                finish(c, weave("z2_woven%d" % c, planes, count, nc.vector.tensor_copy))
-            else:
-                upcoming = weave("z2_woven%d" % c, planes, count, nc.scalar.copy)
-                if c:
-                    finish(c - 1, woven)
-                woven = upcoming
+                finish(c - 1, woven[c - 1])
+            weave(woven[c][:], planes, 0, count, nc.vector.tensor_copy if last else nc.scalar.copy)
+            if last:
+                finish(c, woven[c])
+            elif c:
+                finish(c - 1, woven[c - 1])

@@ -145,8 +145,7 @@ def tile_picked_topdn2_relu_p_kernel(tc, x_words, x_scales, w1, w2, w3, w4, w5, 
 
         w3_bf16 = sbuf("w3_bf16", PACK * H, BF16)
         cast_dealt(w3_bf16[:], w3_low, 0, half)
-        y = [sbuf("y0", 2 * S, F32, "w3_low")] + y
-        nc.gpsimd.memset(y[0][:, S:], 0.0)
+        y = [w3_low] + y
         y_banks = banks(0)
         for t in range(PACK):
             product(y_banks[t], w1_mx, t * P, roots, 0, S, True, True)
@@ -158,15 +157,16 @@ def tile_picked_topdn2_relu_p_kernel(tc, x_words, x_scales, w1, w2, w3, w4, w5, 
 
         z_planes = fetch("z_planes", y, par_sb, 0, V)
         w3_mx = quantise("w3", w3_bf16[:], H)
-        leaf_words = [pick("leaf_words", word_table, U32, leaf_sb[:, : W // 2 // LIST_ROWS], W // 2, "w2_low")]
+        leaf_words = [pick("leaf_words", word_table, U32, leaf_sb[:, :16], 256, "w2_low")]
         w2_mx = quantise("w2", w2_bf16[:], H)
 
         h = [sbuf("h%d" % t, V, F32) for t in range(PACK)]
-        z_woven = sbuf("z_woven", PACK * V, BF16, "w2_high")
         for c, (first, count) in enumerate(NODE_CHUNKS):
-            woven = z_woven[:, PACK * first : PACK * (first + count)]
-            weave(woven, z_planes, first, count, nc.scalar.copy)
-            z = quantise("z%d" % c, woven, count)
+            woven = sbuf("z_woven", PACK * count, BF16, ["w2_high", "w2_bf16"][c])
+            weave(woven[:], z_planes, first, count, nc.scalar.copy)
+            z = quantise("z%d" % c, woven[:], count)
+            if c == 0:
+                leaf_words.append(pick("leaf_words", word_table, U32, leaf_sb[:, 16:32], 256, "w2_high"))
             h_banks = banks(4 - 4 * c)
             for t in range(PACK):
                 product(h_banks[t], w3_mx, t * P, owns, first, count, True, False)
@@ -186,7 +186,7 @@ def tile_picked_topdn2_relu_p_kernel(tc, x_words, x_scales, w1, w2, w3, w4, w5, 
             first, count = LEAF_CHUNKS[c]
             last = c == len(LEAF_CHUNKS) - 1
             z2 = quantise("z2_%d" % c, woven[:], count)
-            leaves = (leaf_words[first // 512][:, first % 512 :], leaf_bytes[:, first:])
+            leaves = (leaf_words[min(c, 2)][:, max(first - 512, 0) :], leaf_bytes[:, first:])
             out_banks = banks(4 - 4 * (c % 2))
             for t in range(PACK):
                 product(out_banks[t], w45_mx, H + t * P, leaves, 0, count, True, False)
@@ -203,8 +203,8 @@ def tile_picked_topdn2_relu_p_kernel(tc, x_words, x_scales, w1, w2, w3, w4, w5, 
         woven = []
         for c, (first, count) in enumerate(LEAF_CHUNKS):
             last = c == len(LEAF_CHUNKS) - 1
-            planes = fetch("z2_planes", h, par2_sb, first, count, ["z2_planes", "w4_raw"][c % 2])
-            woven.append(sbuf("z2_woven%d" % c, PACK * count, BF16))
+            planes = fetch("z2_planes", h, par2_sb, first, count, "z2_planes%d" % (c % 2))
+            woven.append(sbuf("z2_woven%d" % c, PACK * count, BF16, ["w5_raw", None, "z2_0_codes", "z2_1_codes", None][c]))
             if last:
                 finish(c - 1, woven[c - 1])
             weave(woven[c][:], planes, 0, count, nc.vector.tensor_copy if last else nc.scalar.copy)

@@ -10,20 +10,23 @@ U16 = mybir.dt.uint16
 U8 = mybir.dt.uint8
 FP8X4 = mybir.dt.float8_e4m3fn_x4
 RELU = mybir.ActivationFunctionType.Relu
-MULT = mybir.AluOpType.mult
-ADD = mybir.AluOpType.add
 
 P = 128
 PACK = 4
-T, S, V, W, H = 2048, 512, 512, 1024, 512
+QUADRANT = 32
 LIST_ROWS = 16
-FLOPS = 2 * 512 * 512 * (S + 2 * V + 2 * W)
+BANK = 512
+T, S, V, W = 2048, 512, 512, 1024
+H = 512
+FLOPS = 2 * H * H * (S + 2 * V + 2 * W)
 
 NODE_CHUNKS = [(0, 256), (256, 256)]
 LEAF_CHUNKS = [(0, 256), (256, 256), (512, 256), (768, 128), (896, 128)]
 
 
-def tile_picked_topdn2_relu_p_kernel(tc, x_words, x_scales, w1, w2, w3, w4, w5, offs, par, own, par2, leaf, out):
+def tile_picked_topdn2_relu_p_kernel(
+    tc, x_words, x_scales, w1, w2, w3, w4, w5, offs, par, own, par2, leaf, out
+):
     nc = tc.nc
     with ExitStack() as ctx:
         lists = ctx.enter_context(tc.tile_pool(name="lists", bufs=1))
@@ -44,29 +47,17 @@ def tile_picked_topdn2_relu_p_kernel(tc, x_words, x_scales, w1, w2, w3, w4, w5, 
             nc.sync.dma_start(rows, source.rearrange("(p j) c -> p j c", j=PACK)[:, :, first : first + count])
             return tile
 
-        def cast_dealt(target, raw, first, count):
+        def round_dealt(target, raw, first, count):
             nc.scalar.copy(
                 target.rearrange("p (t m j) -> p m j t", t=PACK, j=PACK)[:, first // PACK : (first + count) // PACK],
                 raw[:].rearrange("p (j m t) -> p m j t", j=PACK, t=PACK),
             )
 
-        def cast_plain(target, raw, copy):
-            copy(
+        def round_plain(target, raw):
+            nc.scalar.copy(
                 target.rearrange("p (c i j) -> p c j i", i=PACK, j=PACK),
                 raw[:].rearrange("p (j c i) -> p c j i", j=PACK, i=PACK),
             )
-
-        def cast_pool(target, raw):
-            for piece in range(4):
-                cols = slice(piece * 128, (piece + 1) * 128)
-                nc.gpsimd.tensor_scalar(
-                    target.rearrange("p (c j) -> p c j", j=PACK)[:, cols],
-                    raw[:].rearrange("p (j c) -> p c j", j=PACK)[:, cols],
-                    1.0,
-                    0.0,
-                    MULT,
-                    ADD,
-                )
 
         def quantise(name, values, width):
             codes = sbuf(name + "_codes", width, U32)
@@ -104,16 +95,17 @@ def tile_picked_topdn2_relu_p_kernel(tc, x_words, x_scales, w1, w2, w3, w4, w5, 
             )
 
         def banks(first):
-            return [psum.tile([P, 512], F32, name="bank", tag="bank%d" % (first + t)) for t in range(PACK)]
+            return [psum.tile([P, BANK], F32, name="bank", tag="bank%d" % (first + t)) for t in range(PACK)]
 
         half = H // 2
         byte_table = sbuf("byte_table", T, U8)
         nc.vector.memset(byte_table[:].bitcast(I32), 0)
         offs_sb = load_list("offs_sb", offs)
         leaf_sb = load_list("leaf_sb", leaf)
-        for q in range(4):
+        for q in range(P // QUADRANT):
             nc.sync.dma_start(
-                byte_table[32 * q : 32 * q + 4, :].bitcast(I32), x_scales[0, 4 * q : 4 * q + 4, :].bitcast(I32)
+                byte_table[QUADRANT * q : QUADRANT * q + PACK, :].bitcast(I32),
+                x_scales[0, PACK * q : PACK * (q + 1), :].bitcast(I32),
             )
         w1_low = load_weight("w1_low", w1, 0, half)
         w1_high = load_weight("w1_high", w1, half, half)
@@ -137,78 +129,82 @@ def tile_picked_topdn2_relu_p_kernel(tc, x_words, x_scales, w1, w2, w3, w4, w5, 
         leaf_bytes = pick("leaf_bytes", byte_table, U8, leaf_sb[:], W)
         own_bytes = pick("own_bytes", byte_table, U8, own_sb[:], V)
         w1_bf16 = sbuf("w1_bf16", PACK * H, BF16)
-        cast_dealt(w1_bf16[:], w1_low, 0, half)
-        cast_dealt(w1_bf16[:], w1_high, half, half)
+        round_dealt(w1_bf16[:], w1_low, 0, half)
+        round_dealt(w1_bf16[:], w1_high, half, half)
         w1_mx = quantise("w1", w1_bf16[:], H)
         roots = (pick("root_words", word_table, U32, offs_sb[:], S), root_bytes)
         owns = (pick("own_words", word_table, U32, own_sb[:], V), own_bytes)
 
         w3_bf16 = sbuf("w3_bf16", PACK * H, BF16)
-        cast_dealt(w3_bf16[:], w3_low, 0, half)
+        round_dealt(w3_bf16[:], w3_low, 0, half)
         y = [w3_low] + y
         y_banks = banks(0)
         for t in range(PACK):
             product(y_banks[t], w1_mx, t * P, roots, 0, S, True, True)
             nc.scalar.copy(y[t][:, :S], y_banks[t][:])
-        cast_dealt(w3_bf16[:], w3_high, half, half)
+        round_dealt(w3_bf16[:], w3_high, half, half)
         w2_bf16 = sbuf("w2_bf16", PACK * H, BF16)
-        cast_dealt(w2_bf16[:], w2_low, 0, half)
-        cast_dealt(w2_bf16[:], w2_high, half, half)
+        round_dealt(w2_bf16[:], w2_low, 0, half)
+        round_dealt(w2_bf16[:], w2_high, half, half)
 
         z_planes = fetch("z_planes", y, par_sb, 0, V)
         w3_mx = quantise("w3", w3_bf16[:], H)
-        leaf_words = [pick("leaf_words", word_table, U32, leaf_sb[:, :16], 256, "w2_low")]
+        leaf_half = W // 2
+        leaf_words = [pick("leaf_words", word_table, U32, leaf_sb[:, : leaf_half // LIST_ROWS], leaf_half, "w2_low")]
         w2_mx = quantise("w2", w2_bf16[:], H)
 
         h = [sbuf("h%d" % t, V, F32) for t in range(PACK)]
+        z_woven = sbuf("z_woven", PACK * V, BF16, "w2_high")
         for c, (first, count) in enumerate(NODE_CHUNKS):
-            woven = sbuf("z_woven", PACK * count, BF16, ["w2_high", "w2_bf16"][c])
-            weave(woven[:], z_planes, first, count, nc.scalar.copy)
-            z = quantise("z%d" % c, woven[:], count)
-            if c == 0:
-                leaf_words.append(pick("leaf_words", word_table, U32, leaf_sb[:, 16:32], 256, "w2_high"))
-            h_banks = banks(4 - 4 * c)
+            z_chunk = z_woven[:, PACK * first : PACK * (first + count)]
+            weave(z_chunk, z_planes, first, count, nc.scalar.copy)
+            z = quantise("z%d" % c, z_chunk, count)
+            h_banks = banks(PACK * (1 - c))
             for t in range(PACK):
                 product(h_banks[t], w3_mx, t * P, owns, first, count, True, False)
             for t in range(PACK):
                 product(h_banks[t], w2_mx, t * P, z, 0, count, False, True)
                 nc.scalar.activation(h[t][:, first : first + count], h_banks[t][:, :count], RELU)
 
-        leaf_words.append(pick("leaf_words", word_table, U32, leaf_sb[:, W // 2 // LIST_ROWS :], W // 2, "z_planes"))
+        leaf_words.append(
+            pick("leaf_words", word_table, U32, leaf_sb[:, leaf_half // LIST_ROWS :], leaf_half, "z_planes")
+        )
+
         w45_bf16 = sbuf("w45_bf16", 2 * PACK * H, BF16, "z1_codes")
-        cast_plain(w45_bf16[:, : PACK * H], w4_raw, nc.scalar.copy)
-        cast_plain(w45_bf16[:, PACK * H :], w5_raw, nc.scalar.copy)
+        round_plain(w45_bf16[:, : PACK * H], w4_raw)
+        round_plain(w45_bf16[:, PACK * H :], w5_raw)
         w45_mx = quantise("w45", w45_bf16[:], 2 * H)
 
         out_rows = out.rearrange("(t p) q -> p t q", p=P)
+        last = len(LEAF_CHUNKS) - 1
 
-        def finish(c, woven):
+        def finish(c, z2_chunk):
             first, count = LEAF_CHUNKS[c]
-            last = c == len(LEAF_CHUNKS) - 1
-            z2 = quantise("z2_%d" % c, woven[:], count)
-            leaves = (leaf_words[min(c, 2)][:, max(first - 512, 0) :], leaf_bytes[:, first:])
-            out_banks = banks(4 - 4 * (c % 2))
+            z2 = quantise("z2_%d" % c, z2_chunk[:], count)
+            leaves = (leaf_words[first // leaf_half][:, first % leaf_half :], leaf_bytes[:, first:])
+            out_banks = banks(PACK * (1 - c % 2))
             for t in range(PACK):
                 product(out_banks[t], w45_mx, H + t * P, leaves, 0, count, True, False)
             result = keep.tile([P, PACK, count], F32, name="result%d" % c)
             for t in range(PACK):
                 product(out_banks[t], w45_mx, t * P, z2, 0, count, False, True)
-                copy = nc.vector.tensor_copy if last and t % 2 else nc.scalar.copy
+                shared = c == last and t % 2
+                copy = nc.vector.tensor_copy if shared else nc.scalar.copy
                 copy(result[:, t, :], out_banks[t][:, :count])
-                if last and t % 2:
+                if shared:
                     nc.sync.dma_start(out_rows[:, t - 1 : t + 1, first : first + count], result[:, t - 1 : t + 1, :])
-            if not last:
+            if c != last:
                 nc.sync.dma_start(out_rows[:, :, first : first + count], result[:])
 
-        woven = []
+        z2_woven = []
         for c, (first, count) in enumerate(LEAF_CHUNKS):
-            last = c == len(LEAF_CHUNKS) - 1
-            planes = fetch("z2_planes", h, par2_sb, first, count, "z2_planes%d" % (c % 2))
-            woven.append(sbuf("z2_woven%d" % c, PACK * count, BF16, ["w5_raw", None, "z2_0_codes", "z2_1_codes", None][c]))
-            if last:
-                finish(c - 1, woven[c - 1])
-            weave(woven[c][:], planes, 0, count, nc.vector.tensor_copy if last else nc.scalar.copy)
-            if last:
-                finish(c, woven[c])
-            elif c:
-                finish(c - 1, woven[c - 1])
+            z2_planes = fetch("z2_planes", h, par2_sb, first, count, ["z2_planes", "w4_raw"][c % 2])
+            z2_woven.append(sbuf("z2_woven%d" % c, PACK * count, BF16))
+            if c == last:
+                finish(c - 1, z2_woven[c - 1])
+                weave(z2_woven[c][:], z2_planes, 0, count, nc.vector.tensor_copy)
+                finish(c, z2_woven[c])
+            else:
+                weave(z2_woven[c][:], z2_planes, 0, count, nc.scalar.copy)
+                if c:
+                    finish(c - 1, z2_woven[c - 1])

from contextlib import ExitStack

import concourse.mybir as mybir

F32 = mybir.dt.float32
BF16 = mybir.dt.bfloat16
I32 = mybir.dt.int32
U32 = mybir.dt.uint32
U16 = mybir.dt.uint16
U8 = mybir.dt.uint8
FP8X4 = mybir.dt.float8_e4m3fn_x4
RELU = mybir.ActivationFunctionType.Relu

P = 128
PACK = 4
QUADRANT = 32
LIST_ROWS = 16
BANK = 512
T, S, V, W = 2048, 512, 512, 1024
H = 512
FLOPS = 2 * H * H * (S + 2 * V + 2 * W)

NODE_CHUNKS = [(0, 256), (256, 256)]
LEAF_CHUNKS = [(0, 256), (256, 256), (512, 256), (768, 128), (896, 128)]


def tile_picked_topdn2_relu_p_kernel(
    tc, x_words, x_scales, w1, w2, w3, w4, w5, offs, par, own, par2, leaf, out
):
    nc = tc.nc
    with ExitStack() as ctx:
        lists = ctx.enter_context(tc.tile_pool(name="lists", bufs=1))
        keep = ctx.enter_context(tc.tile_pool(name="keep", bufs=1))
        psum = ctx.enter_context(tc.psum_pool(name="psum", bufs=1))

        def sbuf(name, width, dtype, slot=None):
            return keep.tile([P, width], dtype, name=name, tag=slot or name, align_bytes=64)

        def load_list(name, source):
            tile = lists.tile(list(source.shape), U16, name=name)
            nc.sync.dma_start(tile[:], source)
            return tile

        def load_weight(name, source, first, count):
            tile = sbuf(name, PACK * count, F32)
            rows = tile[:].rearrange("p (j c) -> p j c", j=PACK)
            nc.sync.dma_start(rows, source.rearrange("(p j) c -> p j c", j=PACK)[:, :, first : first + count])
            return tile

        def round_dealt(target, raw, first, count):
            nc.scalar.copy(
                target.rearrange("p (t m j) -> p m j t", t=PACK, j=PACK)[:, first // PACK : (first + count) // PACK],
                raw[:].rearrange("p (j m t) -> p m j t", j=PACK, t=PACK),
            )

        def round_plain(target, raw):
            nc.scalar.copy(
                target.rearrange("p (c i j) -> p c j i", i=PACK, j=PACK),
                raw[:].rearrange("p (j c i) -> p c j i", j=PACK, i=PACK),
            )

        def quantise(name, values, width):
            codes = sbuf(name + "_codes", width, U32)
            scales = sbuf(name + "_scales", width, U8)
            nc.vector.quantize_mx(out=codes[:].bitcast(FP8X4), scales=scales[:], in_=values)
            return codes, scales

        def pick(name, table, dtype, offsets, count, slot=None):
            tile = sbuf(name, count, dtype, slot)
            nc.vector.tensor_copy(tile[:], table[:].indirect(offsets))
            return tile

        def fetch(name, rows, offsets, first, count, slot=None):
            planes = sbuf(name, PACK * count, BF16, slot)
            entries = offsets[:, first // LIST_ROWS : (first + count) // LIST_ROWS]
            for t in range(PACK):
                nc.vector.tensor_copy(planes[:, t * count : (t + 1) * count], rows[t][:].indirect(entries))
            return planes

        def weave(target, planes, first, count, copy):
            copy(
                target.rearrange("p (c i t) -> p c t i", i=PACK, t=PACK),
                planes[:].rearrange("p (t c i) -> p c t i", t=PACK, i=PACK)[:, first // PACK : (first + count) // PACK],
            )

        def product(bank, weights, column, moving, first, count, start, stop):
            nc.tensor.matmul_mx(
                out=bank[:, :count],
                lhsT=weights[0][:, column : column + P].bitcast(FP8X4),
                lhsT_scale=weights[1][:, column : column + P],
                rhs=moving[0][:, first : first + count].bitcast(FP8X4),
                rhs_scale=moving[1][:, first : first + count],
                start=start,
                stop=stop,
            )

        def banks(first):
            return [psum.tile([P, BANK], F32, name="bank", tag="bank%d" % (first + t)) for t in range(PACK)]

        half = H // 2
        byte_table = sbuf("byte_table", T, U8)
        nc.vector.memset(byte_table[:].bitcast(I32), 0)
        offs_sb = load_list("offs_sb", offs)
        leaf_sb = load_list("leaf_sb", leaf)
        for q in range(P // QUADRANT):
            nc.sync.dma_start(
                byte_table[QUADRANT * q : QUADRANT * q + PACK, :].bitcast(I32),
                x_scales[0, PACK * q : PACK * (q + 1), :].bitcast(I32),
            )
        w1_low = load_weight("w1_low", w1, 0, half)
        w1_high = load_weight("w1_high", w1, half, half)
        own_sb = load_list("own_sb", own)
        word_table = sbuf("word_table", T, U32)
        nc.sync.dma_start(word_table[:].bitcast(I32), x_words[0].rearrange("p n r -> p (n r)").bitcast(I32))
        w3_low = load_weight("w3_low", w3, 0, half)
        w3_high = load_weight("w3_high", w3, half, half)
        par_sb = load_list("par_sb", par)
        w2_low = load_weight("w2_low", w2, 0, half)
        w2_high = load_weight("w2_high", w2, half, half)
        par2_sb = load_list("par2_sb", par2)
        w4_raw = load_weight("w4_raw", w4, 0, H)
        w5_raw = load_weight("w5_raw", w5, 0, H)

        y = [sbuf("y%d" % t, 2 * S, F32) for t in range(1, PACK)]
        for rows in y:
            nc.vector.memset(rows[:, S:], 0.0)

        root_bytes = pick("root_bytes", byte_table, U8, offs_sb[:], S)
        leaf_bytes = pick("leaf_bytes", byte_table, U8, leaf_sb[:], W)
        own_bytes = pick("own_bytes", byte_table, U8, own_sb[:], V)
        w1_bf16 = sbuf("w1_bf16", PACK * H, BF16)
        round_dealt(w1_bf16[:], w1_low, 0, half)
        round_dealt(w1_bf16[:], w1_high, half, half)
        w1_mx = quantise("w1", w1_bf16[:], H)
        roots = (pick("root_words", word_table, U32, offs_sb[:], S), root_bytes)
        owns = (pick("own_words", word_table, U32, own_sb[:], V), own_bytes)

        w3_bf16 = sbuf("w3_bf16", PACK * H, BF16)
        round_dealt(w3_bf16[:], w3_low, 0, half)
        y = [w3_low] + y
        y_banks = banks(0)
        for t in range(PACK):
            product(y_banks[t], w1_mx, t * P, roots, 0, S, True, True)
            nc.scalar.copy(y[t][:, :S], y_banks[t][:])
        round_dealt(w3_bf16[:], w3_high, half, half)
        w2_bf16 = sbuf("w2_bf16", PACK * H, BF16)
        round_dealt(w2_bf16[:], w2_low, 0, half)
        round_dealt(w2_bf16[:], w2_high, half, half)

        z_planes = fetch("z_planes", y, par_sb, 0, V)
        w3_mx = quantise("w3", w3_bf16[:], H)
        leaf_half = W // 2
        leaf_words = [pick("leaf_words", word_table, U32, leaf_sb[:, : leaf_half // LIST_ROWS], leaf_half, "w2_low")]
        w2_mx = quantise("w2", w2_bf16[:], H)

        h = [sbuf("h%d" % t, V, F32) for t in range(PACK)]
        z_woven = sbuf("z_woven", PACK * V, BF16, "w2_high")
        for c, (first, count) in enumerate(NODE_CHUNKS):
            z_chunk = z_woven[:, PACK * first : PACK * (first + count)]
            weave(z_chunk, z_planes, first, count, nc.scalar.copy)
            z = quantise("z%d" % c, z_chunk, count)
            h_banks = banks(PACK * (1 - c))
            for t in range(PACK):
                product(h_banks[t], w3_mx, t * P, owns, first, count, True, False)
            for t in range(PACK):
                product(h_banks[t], w2_mx, t * P, z, 0, count, False, True)
                nc.scalar.activation(h[t][:, first : first + count], h_banks[t][:, :count], RELU)

        leaf_words.append(
            pick("leaf_words", word_table, U32, leaf_sb[:, leaf_half // LIST_ROWS :], leaf_half, "z_planes")
        )

        w45_bf16 = sbuf("w45_bf16", 2 * PACK * H, BF16, "z1_codes")
        round_plain(w45_bf16[:, : PACK * H], w4_raw)
        round_plain(w45_bf16[:, PACK * H :], w5_raw)
        w45_mx = quantise("w45", w45_bf16[:], 2 * H)

        out_rows = out.rearrange("(t p) q -> p t q", p=P)
        last = len(LEAF_CHUNKS) - 1

        def finish(c, z2_chunk):
            first, count = LEAF_CHUNKS[c]
            z2 = quantise("z2_%d" % c, z2_chunk[:], count)
            leaves = (leaf_words[first // leaf_half][:, first % leaf_half :], leaf_bytes[:, first:])
            out_banks = banks(PACK * (1 - c % 2))
            for t in range(PACK):
                product(out_banks[t], w45_mx, H + t * P, leaves, 0, count, True, False)
            result = keep.tile([P, PACK, count], F32, name="result%d" % c)
            for t in range(PACK):
                product(out_banks[t], w45_mx, t * P, z2, 0, count, False, True)
                shared = c == last and t % 2
                copy = nc.vector.tensor_copy if shared else nc.scalar.copy
                copy(result[:, t, :], out_banks[t][:, :count])
                if shared:
                    nc.sync.dma_start(out_rows[:, t - 1 : t + 1, first : first + count], result[:, t - 1 : t + 1, :])
            if c != last:
                nc.sync.dma_start(out_rows[:, :, first : first + count], result[:])

        z2_woven = []
        for c, (first, count) in enumerate(LEAF_CHUNKS):
            z2_planes = fetch("z2_planes", h, par2_sb, first, count, ["z2_planes", "w4_raw"][c % 2])
            z2_woven.append(sbuf("z2_woven%d" % c, PACK * count, BF16))
            if c == last:
                finish(c - 1, z2_woven[c - 1])
                weave(z2_woven[c][:], z2_planes, 0, count, nc.vector.tensor_copy)
                finish(c, z2_woven[c])
            else:
                weave(z2_woven[c][:], z2_planes, 0, count, nc.scalar.copy)
                if c:
                    finish(c - 1, z2_woven[c - 1])
